import numpy as np
import ml_dtypes


def mxq(x, axis, fmt="e4m3"):
    dtype, down = {"e4m3": (ml_dtypes.float8_e4m3fn, 7), "e5m2": (ml_dtypes.float8_e5m2, 14)}[fmt]
    v = np.moveaxis(np.asarray(x, np.float32).astype(ml_dtypes.bfloat16).astype(np.float64), axis, -1)
    blocks = v.reshape(v.shape[:-1] + (-1, 32))
    amax = np.abs(blocks).max(-1, keepdims=True)
    byte = np.maximum(np.where(amax > 0, np.frexp(amax)[1] - 1 + 127, 0) - down, 1)
    scale = np.exp2(byte - 127.0)
    codes = (blocks / scale).astype(np.float32).astype(dtype).astype(np.float64)
    return np.moveaxis((codes * scale).reshape(v.shape), -1, axis)


WIDE = False


def mx_kscale(k):
    if not WIDE:
        return np.ones(k)
    levels = np.array([10, -10, 5, -5, 0])
    if k % 512:
        return np.exp2(np.random.permutation(np.resize(levels, k // 32))).repeat(32)
    a = np.empty((k // 512, 16))
    for p in range(k // 512):
        a[p, :8] = np.random.permutation(np.resize(levels, 8))
        for g in range(8):
            far = levels[np.abs(levels - a[p, g]) >= 10]
            a[p, g + 8] = far[np.random.randint(len(far))]
    return np.exp2(a.ravel()).repeat(32)


def f64(x):
    return np.asarray(x).astype(np.float64)


def striped(idx):
    return np.tile(idx.reshape(-1, 16).T, (8, 1)).astype(np.uint16)


def unstriped(offs):
    return offs[:16].T.reshape(-1).astype(np.int64)


E2M1 = np.array([0.0, 0.5, 1.0, 1.5, 2.0, 3.0, 4.0, 6.0, -0.0, -0.5, -1.0, -1.5, -2.0, -3.0, -4.0, -6.0])


def pack_weight(w, fmt):
    k, n = w.shape
    w = f64(np.asarray(w, np.float32).astype(ml_dtypes.bfloat16)).reshape(k // 32, 32, n)
    amax = np.abs(w).max(1)
    if fmt == "e4m3":
        byte = np.frexp(amax)[1] - 1 + 127 - 7
    else:
        mant, ex = np.frexp(amax / 6.0)
        byte = np.where(mant > 0.5, ex, ex - 1) + 127
    byte = np.clip(np.where(amax > 0, byte, 1), 1, 254)
    scaled = (w * np.exp2(127.0 - byte)[:, None, :]).reshape(k, n).astype(np.float32)
    by_word = np.ascontiguousarray(scaled.reshape(k // 512, 128, 4, n).transpose(0, 1, 3, 2))
    if fmt == "e4m3":
        words = by_word.astype(ml_dtypes.float8_e4m3fn).view(np.uint8)
    else:
        c = by_word.astype(ml_dtypes.float4_e2m1fn).view(np.uint8) & 0xF
        words = (c[..., 0::2] | (c[..., 1::2] << 4)).reshape(k // 512, 128, 2 * n)
    return np.ascontiguousarray(words), np.ascontiguousarray(byte.astype(np.uint8).reshape(k // 512, 16, n))


def unpack_weight(words, scales, fmt):
    g, _, n = scales.shape
    words = np.ascontiguousarray(words).reshape(g, 128, n, -1)
    if fmt == "e4m3":
        vals = words.view(ml_dtypes.float8_e4m3fn).astype(np.float64)
    else:
        nib = np.empty((g, 128, n, 4), np.uint8)
        nib[..., 0::2] = words & 0xF
        nib[..., 1::2] = words >> 4
        vals = E2M1[nib]
    vals = vals * np.repeat(np.exp2(scales.astype(np.float64) - 127.0), 8, axis=1)[..., None]
    return vals.transpose(0, 1, 3, 2).reshape(g * 512, n)


def gelu(v):
    return 0.5 * v * (1.0 + np.tanh(np.sqrt(2.0 / np.pi) * (v + 0.044715 * v**3)))


def striped8(idx):
    return np.concatenate([v.reshape(-1, 16).T for v in idx]).astype(np.uint16)


def unstriped8(offs):
    return np.stack([offs[16 * g:16 * g + 16].T.reshape(-1) for g in range(8)]).astype(np.int64)


def heads(h, wgt, idx8):
    r = np.arange(h.shape[0])
    return wgt[r // 4 % 128] * h[r[:, None], idx8[r % 512 // 64]]


K, T, S, H, T2, P, N = 1024, 4096, 1024, 512, 2048, 1024, 512

def setup_inputs():
    n = np.random.standard_normal
    s = mx_kscale(K)[:, None]
    u = mx_kscale(H)[:, None]
    tab_words, tab_scales = pack_weight(n((K, T)) * s, "e4m3")
    w1 = n((K, H)) / np.sqrt(K) / s * u.T
    w4_words, w4_scales = pack_weight(n((K, H)) / np.sqrt(K) / s * u.T, "e2m1")
    w2 = n((H, N)) / np.sqrt(H) / u
    w5_words, w5_scales = pack_weight(n((H, N)) / np.sqrt(H) / u, "e4m3")
    cells = np.stack([np.random.permutation(T2)[:P] for _ in range(8)])
    return {
        "tab_words": tab_words, "tab_scales": tab_scales,
        "offs": striped(np.random.permutation(T)[:S]),
        "w1": w1.astype(np.float32),
        "w4_words": w4_words, "w4_scales": w4_scales,
        "d": (0.7 * n(H) * u[:, 0]).astype(np.float32),
        "page0": (n((H, T2)) * u).astype(np.float32),
        "wgs": np.exp(0.3 * n((128, S))).astype(np.float32),
        "offs2": striped(np.random.permutation(T2)[:S]),
        "wgt": np.repeat(np.random.uniform(0.5, 2.0, (8, P)), 16, axis=0).astype(np.float32),
        "offs3": striped8(cells),
        "w2": w2.astype(np.float32),
        "w5_words": w5_words, "w5_scales": w5_scales,
    }

def reference(tab_words, tab_scales, offs, w1, w4_words, w4_scales, d, page0, wgs, offs2, wgt, offs3, w2, w5_words, w5_scales):
    v = unpack_weight(tab_words, tab_scales, "e4m3")[:, unstriped(offs)]
    w4 = unpack_weight(w4_words, w4_scales, "e2m1")
    w5 = unpack_weight(w5_words, w5_scales, "e4m3")
    a = mxq(f64(w1), 0, "e4m3").T @ v
    b = w4.T @ v
    h = np.maximum(a, b) + f64(d)[:, None]
    page = f64(page0).copy()
    page[:, unstriped(offs2)] = np.tile(f64(wgs), (H // 128, 1)) * h
    x = heads(page, f64(wgt), unstriped8(offs3))
    xq = mxq(x, 0, "e4m3")
    return np.maximum(mxq(f64(w2), 0, "e4m3").T @ xq, w5.T @ xq)

@@ -1,0 +1,233 @@
+from contextlib import ExitStack
+
+import concourse.mybir as mybir
+
+K, T, S, H, T2, M, N = 1024, 4096, 1024, 512, 2048, 1024, 512
+FLOPS = 2 * (2 * K * H * S + 2 * H * N * M)
+
+F32 = mybir.dt.float32
+BF16 = mybir.dt.bfloat16
+I32 = mybir.dt.int32
+U32 = mybir.dt.uint32
+U16 = mybir.dt.uint16
+U8 = mybir.dt.uint8
+FP8X4 = mybir.dt.float8_e4m3fn_x4
+FP4X4 = mybir.dt.float4_e2m1fn_x4
+MULT = mybir.AluOpType.mult
+MAX = mybir.AluOpType.max
+IDENTITY = mybir.ActivationFunctionType.Identity
+
+P = 128
+PACK = 4
+PASSES = K // (P * PACK)
+BANK = 512
+CHUNKS = (256, 256, 256, 256)
+
+
+def tile_list_corridor_cell_limits_kernel(
+    tc, tab_words, tab_scales, offs, w1, w4_words, w4_scales, d, page0, wgs, offs2, wgt, offs3,
+    w2, w5_words, w5_scales, out,
+):
+    nc = tc.nc
+    with ExitStack() as ctx:
+        keep = ctx.enter_context(tc.tile_pool(name="keep", bufs=1))
+        swap = ctx.enter_context(tc.tile_pool(name="swap", bufs=1))
+        ring = ctx.enter_context(tc.tile_pool(name="ring", bufs=3))
+        outs = ctx.enter_context(tc.tile_pool(name="outs", bufs=8))
+        psum = ctx.enter_context(tc.psum_pool(name="psum", bufs=4))
+
+        def held(name, shape, dtype):
+            return keep.tile(shape, dtype, name=name, align_bytes=64)
+
+        idx = held("idx", [P, S // 16], U16)
+        idx2 = held("idx2", [P, S // 16], U16)
+        idx3 = held("idx3", [P, M // 16], U16)
+        tab = [held("tab%d" % a, [P, T], U32) for a in range(PASSES)]
+        tab_sc = held("tab_sc", [P, T], U8)
+        v_words = [held("v_words%d" % a, [P, S], U32) for a in range(PASSES)]
+        v_sc_rows = held("v_sc_rows", [P, S], U8)
+        v_sc = held("v_sc", [P, PASSES * S], U8)
+        w4_raw = held("w4_raw", [P, PASSES * H], U16)
+        w4_sc_raw = held("w4_sc_raw", [P, PASSES * H], U8)
+        w4_codes = held("w4_codes", [P, PASSES * H], U16)
+        w4_sc = held("w4_sc", [P, PASSES * H], U8)
+        w1_raw = [held("w1_raw%d" % a, [P, PACK, H], F32) for a in range(PASSES)]
+        w1_bf = [held("w1_bf%d" % a, [P, PACK * H], BF16) for a in range(PASSES)]
+        w1_codes = [held("w1_codes%d" % a, [P, H], U32) for a in range(PASSES)]
+        w1_sc = [held("w1_sc%d" % a, [P, H], U8) for a in range(PASSES)]
+        d_sb = held("d_sb", [P, PACK], F32)
+        page = [held("page%d" % t, [P, T2], F32) for t in range(PACK)]
+        wgs_first = held("wgs_first", [P, S], F32)
+        wgs_rest = held("wgs_rest", [P, (PACK - 1) * S], F32)
+        wgt_sb = held("wgt_sb", [P, M], F32)
+        w2_raw = held("w2_raw", [P, PACK, N], F32)
+        w2_bf = held("w2_bf", [P, PACK * N], BF16)
+        w2_codes = held("w2_codes", [P, N], U32)
+        w2_sc = held("w2_sc", [P, N], U8)
+        w5_codes = held("w5_codes", [P, N], U32)
+        w5_sc = held("w5_sc", [P, N], U8)
+        b_sb = [held("b_sb%d" % u, [P, BANK], F32) for u in range(PACK * S // BANK)]
+        h_sb = swap.tile([P, PACK * S], F32, name="h_sb", offset=0)
+
+        nc.vector.memset(w4_sc_raw[:].bitcast(I32), 0)
+        nc.vector.memset(tab_sc[32:64, :].bitcast(I32), 0)
+        nc.vector.memset(tab_sc[64:128, :].bitcast(I32), 0)
+        for plane in (v_sc, w5_sc):
+            nc.vector.memset(plane[:].bitcast(I32), 0)
+
+        nc.sync.dma_start(idx[:], offs)
+
+        def load_tab(a):
+            nc.sync.dma_start(tab[a][:].bitcast(I32), tab_words[a].rearrange("p t i -> p (t i)").bitcast(I32))
+
+        nc.sync.dma_start(
+            tab_sc[0:32, :].bitcast(I32), tab_scales.bitcast(I32).rearrange("a q t -> q a t")
+        )
+        nc.sync.dma_start(
+            w4_raw[:].bitcast(I32).rearrange("p (a c) -> p a c", a=PASSES),
+            w4_words.bitcast(I32).rearrange("a p c -> p a c"),
+        )
+        nc.sync.dma_start(d_sb[:], d.rearrange("(p t) -> p t", t=PACK))
+        for q in range(4):
+            nc.scalar.dma_start(
+                w4_sc_raw[32 * q : 32 * q + 4, :].bitcast(I32).rearrange("r (a c) -> r a c", a=PASSES),
+                w4_scales.bitcast(I32)[:, 4 * q : 4 * q + 4, :].rearrange("a r c -> r a c"),
+            )
+        load_tab(0)
+        load_tab(1)
+        for a in range(PASSES):
+            nc.sync.dma_start(
+                w1_raw[a][:], w1[512 * a : 512 * (a + 1), :].rearrange("(p j) c -> p j c", j=PACK)
+            )
+        wgs_rows = wgs.rearrange("(q t) j -> q (t j)", t=PACK)
+        for q in (0, 2, 1, 3):
+            nc.sync.dma_start(wgs_first[32 * q : 32 * q + 32, :], wgs_rows[:, 0:S])
+        nc.sync.dma_start(idx2[:], offs2)
+        page_rows = page0.rearrange("(p t) c -> t p c", t=PACK)
+        nc.sync.dma_start(page[0][:], page_rows[0])
+        for q in (0, 2, 1, 3):
+            nc.sync.dma_start(wgs_rest[32 * q : 32 * q + 32, :], wgs_rows[:, S : PACK * S])
+        for t in range(1, PACK):
+            nc.sync.dma_start(page[t][:], page_rows[t])
+        nc.sync.dma_start(idx3[:], offs3)
+        nc.sync.dma_start(wgt_sb[:], wgt)
+        nc.sync.dma_start(w2_raw[:], w2.rearrange("(p j) n -> p j n", j=PACK))
+        nc.sync.dma_start(w5_codes[:].bitcast(I32), w5_words[0].rearrange("p c i -> p (c i)").bitcast(I32))
+        for q in range(4):
+            nc.sync.dma_start(
+                w5_sc[32 * q : 32 * q + 4, :].bitcast(I32), w5_scales[0].bitcast(I32)[4 * q : 4 * q + 4, :]
+            )
+
+        nc.vector.tensor_copy(v_sc_rows[:], tab_sc[:].indirect(idx[:]))
+        for q in range(4):
+            nc.gpsimd.dma_start(
+                v_sc[32 * q : 32 * q + 4, :].bitcast(I32).rearrange("r (a j) -> r a j", a=PASSES),
+                v_sc_rows[8 * q : 8 * q + 8, :].bitcast(I32),
+            )
+        nc.vector.tensor_copy(v_words[0][:], tab[0][:].indirect(idx[:]))
+        nc.vector.tensor_copy(
+            w4_codes[:].rearrange("p (a t m) -> p a m t", a=PASSES, t=PACK),
+            w4_raw[:].rearrange("p (a m t) -> p a m t", a=PASSES, t=PACK),
+        )
+        nc.vector.tensor_copy(
+            w4_sc[:].rearrange("p (a t m) -> p a m t", a=PASSES, t=PACK),
+            w4_sc_raw[:].rearrange("p (a m t) -> p a m t", a=PASSES, t=PACK),
+        )
+        nc.vector.tensor_copy(v_words[1][:], tab[1][:].indirect(idx[:]))
+
+        for a in range(PASSES):
+            nc.vector.tensor_copy(
+                w1_bf[a][:].rearrange("p (t m j) -> p m j t", t=PACK, j=PACK),
+                w1_raw[a][:].rearrange("p j (m t) -> p m j t", t=PACK),
+            )
+            nc.vector.quantize_mx(out=w1_codes[a][:].bitcast(FP8X4), scales=w1_sc[a][:], in_=w1_bf[a][:])
+
+        halves = S // BANK
+        for t in range(PACK):
+            for half in range(halves):
+                acc_b = psum.tile([P, BANK], F32, name="acc_b", tag="second")
+                for a in range(PASSES):
+                    c0 = a * H + t * P
+                    nc.tensor.matmul_mx(
+                        out=acc_b[:],
+                        lhsT=w4_codes[:, c0 : c0 + P].bitcast(FP4X4),
+                        lhsT_scale=w4_sc[:, c0 : c0 + P],
+                        rhs=v_words[a][:, half * BANK : (half + 1) * BANK].bitcast(FP8X4),
+                        rhs_scale=v_sc[:, a * S + half * BANK : a * S + (half + 1) * BANK],
+                        start=(a == 0),
+                        stop=(a == PASSES - 1),
+                    )
+                nc.scalar.copy(b_sb[t * halves + half][:], acc_b[:])
+
+        for t in range(PACK):
+            for half in range(halves):
+                acc_a = psum.tile([P, BANK], F32, name="acc_a", tag="first")
+                for a in range(PASSES):
+                    nc.tensor.matmul_mx(
+                        out=acc_a[:],
+                        lhsT=w1_codes[a][:, t * P : (t + 1) * P].bitcast(FP8X4),
+                        lhsT_scale=w1_sc[a][:, t * P : (t + 1) * P],
+                        rhs=v_words[a][:, half * BANK : (half + 1) * BANK].bitcast(FP8X4),
+                        rhs_scale=v_sc[:, a * S + half * BANK : a * S + (half + 1) * BANK],
+                        start=(a == 0),
+                        stop=(a == PASSES - 1),
+                    )
+                larger = ring.tile([P, BANK], F32, name="larger", tag="stage")
+                nc.vector.tensor_tensor(larger[:], acc_a[:], b_sb[t * halves + half][:], MAX)
+                c0 = t * S + half * BANK
+                nc.scalar.activation(h_sb[:, c0 : c0 + BANK], larger[:], IDENTITY, bias=d_sb[:, t : t + 1])
+
+        for t in range(PACK):
+            weight = wgs_first[:] if t == 0 else wgs_rest[:, (t - 1) * S : t * S]
+            nc.vector.tensor_tensor(page[t][:].indirect(idx2[:]), h_sb[:, t * S : (t + 1) * S], weight, MULT)
+
+        nc.scalar.copy(
+            w2_bf[:].rearrange("p (c i j) -> p c j i", i=4, j=PACK),
+            w2_raw[:].rearrange("p j (c i) -> p c j i", i=4),
+        )
+        nc.vector.quantize_mx(out=w2_codes[:].bitcast(FP8X4), scales=w2_sc[:], in_=w2_bf[:])
+
+        out_rows = out.rearrange("(g p) m -> p g m", p=P)
+        m0 = 0
+        for c, width in enumerate(CHUNKS):
+            picked = swap.tile([P, PACK, width], F32, name="picked%d" % c, offset=4 * PACK * m0)
+            for t in range(PACK):
+                nc.vector.tensor_tensor(
+                    picked[:, t, :],
+                    page[t][:].indirect(idx3[:, m0 // 16 : (m0 + width) // 16]),
+                    wgt_sb[:, m0 : m0 + width],
+                    MULT,
+                )
+            x_bf = held("x_bf%d" % c, [P, PACK * width], BF16)
+            nc.scalar.copy(
+                x_bf[:].rearrange("p (c i t) -> p c t i", i=4, t=PACK),
+                picked[:].rearrange("p t (c i) -> p c t i", i=4),
+            )
+            x_codes = held("x_codes%d" % c, [P, width], U32)
+            x_sc = held("x_sc%d" % c, [P, width], U8)
+            nc.vector.quantize_mx(out=x_codes[:].bitcast(FP8X4), scales=x_sc[:], in_=x_bf[:])
+            per_bank = BANK // width
+            for g0 in range(0, N // P, per_bank):
+                acc_c = psum.tile([P, BANK], F32, name="acc_c", tag="first")
+                acc_e = psum.tile([P, BANK], F32, name="acc_e", tag="second")
+                for acc, codes, scales in ((acc_e, w5_codes, w5_sc), (acc_c, w2_codes, w2_sc)):
+                    for g in range(per_bank):
+                        n0 = (g0 + g) * P
+                        nc.tensor.matmul_mx(
+                            out=acc[:, g * width : (g + 1) * width],
+                            lhsT=codes[:, n0 : n0 + P].bitcast(FP8X4),
+                            lhsT_scale=scales[:, n0 : n0 + P],
+                            rhs=x_codes[:].bitcast(FP8X4),
+                            rhs_scale=x_sc[:],
+                            start=True,
+                            stop=True,
+                        )
+                e_sb = ring.tile([P, BANK], F32, name="e_sb", tag="stage")
+                nc.scalar.copy(e_sb[:], acc_e[:])
+                result = outs.tile([P, BANK], F32, name="result")
+                nc.vector.tensor_tensor(result[:], acc_c[:], e_sb[:], MAX)
+                nc.sync.dma_start(
+                    out_rows[:, g0 : g0 + per_bank, m0 : m0 + width],
+                    result[:].rearrange("p (g m) -> p g m", g=per_bank),
+                )
+            m0 += width

@@ -22,6 +22,11 @@ PACK = 4
 PASSES = K // (P * PACK)
 BANK = 512
 CHUNKS = (256, 256, 256, 256)
+PICKED_AT = (0, 4096, 8192, 12288)
+XBF_AT = (16384, 12288, 18432, 20480)
+EARLY_AT = 22528
+SPLIT = 88
+KB = 1024
 
 
 def tile_list_corridor_cell_limits_kernel(
@@ -32,9 +37,10 @@ def tile_list_corridor_cell_limits_kernel(
     with ExitStack() as ctx:
         keep = ctx.enter_context(tc.tile_pool(name="keep", bufs=1))
         swap = ctx.enter_context(tc.tile_pool(name="swap", bufs=1))
+        reuse = ctx.enter_context(tc.tile_pool(name="reuse", bufs=1))
         ring = ctx.enter_context(tc.tile_pool(name="ring", bufs=3))
         outs = ctx.enter_context(tc.tile_pool(name="outs", bufs=8))
-        psum = ctx.enter_context(tc.psum_pool(name="psum", bufs=4))
+        psum = ctx.enter_context(tc.psum_pool(name="psum", bufs=1))
 
         def held(name, shape, dtype):
             return keep.tile(shape, dtype, name=name, align_bytes=64)
@@ -42,44 +48,37 @@ def tile_list_corridor_cell_limits_kernel(
         idx = held("idx", [P, S // 16], U16)
         idx2 = held("idx2", [P, S // 16], U16)
         idx3 = held("idx3", [P, M // 16], U16)
-        tab = [held("tab%d" % a, [P, T], U32) for a in range(PASSES)]
-        tab_sc = held("tab_sc", [P, T], U8)
+        def placed(name, shape, dtype, offset):
+            return reuse.tile(shape, dtype, name=name, align_bytes=64, offset=offset)
+
+        tab = [placed("tab%d" % a, [P, T], U32, 4 * T * a) for a in range(PASSES)]
+        tab_sc = placed("tab_sc", [P, T], U8, 38 * KB)
         v_words = [held("v_words%d" % a, [P, S], U32) for a in range(PASSES)]
         v_sc_rows = held("v_sc_rows", [P, S], U8)
         v_sc = held("v_sc", [P, PASSES * S], U8)
-        w4_raw = held("w4_raw", [P, PASSES * H], U16)
-        w4_sc_raw = held("w4_sc_raw", [P, PASSES * H], U8)
-        w4_codes = held("w4_codes", [P, PASSES * H], U16)
-        w4_sc = held("w4_sc", [P, PASSES * H], U8)
-        w1_raw = [held("w1_raw%d" % a, [P, PACK, H], F32) for a in range(PASSES)]
-        w1_bf = [held("w1_bf%d" % a, [P, PACK * H], BF16) for a in range(PASSES)]
+        w4_raw = placed("w4_raw", [P, PASSES * H], U16, 4 * T)
+        w4_sc_raw = swap.tile([P, PASSES * H], U8, name="w4_sc_raw", offset=EARLY_AT, align_bytes=64)
+        w4_codes = placed("w4_codes", [P, PASSES * H], U16, 56 * KB)
+        w4_sc = placed("w4_sc", [P, PASSES * H], U8, 58 * KB)
+        w1_bf = [placed("w1_bf%d" % a, [P, PACK * H], BF16, (48 + 4 * a) * KB) for a in range(PASSES)]
         w1_codes = [held("w1_codes%d" % a, [P, H], U32) for a in range(PASSES)]
         w1_sc = [held("w1_sc%d" % a, [P, H], U8) for a in range(PASSES)]
         d_sb = held("d_sb", [P, PACK], F32)
-        page = [held("page%d" % t, [P, T2], F32) for t in range(PACK)]
-        wgs_first = held("wgs_first", [P, S], F32)
-        wgs_rest = held("wgs_rest", [P, (PACK - 1) * S], F32)
-        wgt_sb = held("wgt_sb", [P, M], F32)
-        w2_raw = held("w2_raw", [P, PACK, N], F32)
         w2_bf = held("w2_bf", [P, PACK * N], BF16)
         w2_codes = held("w2_codes", [P, N], U32)
         w2_sc = held("w2_sc", [P, N], U8)
-        w5_codes = held("w5_codes", [P, N], U32)
-        w5_sc = held("w5_sc", [P, N], U8)
         b_sb = [held("b_sb%d" % u, [P, BANK], F32) for u in range(PACK * S // BANK)]
-        h_sb = swap.tile([P, PACK * S], F32, name="h_sb", offset=0)
+        h_sb = swap.tile([P, PACK * S], F32, name="h_sb", offset=0, align_bytes=64)
 
         nc.vector.memset(w4_sc_raw[:].bitcast(I32), 0)
         nc.vector.memset(tab_sc[32:64, :].bitcast(I32), 0)
         nc.vector.memset(tab_sc[64:128, :].bitcast(I32), 0)
-        for plane in (v_sc, w5_sc):
-            nc.vector.memset(plane[:].bitcast(I32), 0)
-
-        nc.sync.dma_start(idx[:], offs)
+        nc.vector.memset(v_sc[:].bitcast(I32), 0)
 
         def load_tab(a):
             nc.sync.dma_start(tab[a][:].bitcast(I32), tab_words[a].rearrange("p t i -> p (t i)").bitcast(I32))
 
+        nc.sync.dma_start(idx[:], offs)
         nc.sync.dma_start(
             tab_sc[0:32, :].bitcast(I32), tab_scales.bitcast(I32).rearrange("a q t -> q a t")
         )
@@ -88,109 +87,152 @@ def tile_list_corridor_cell_limits_kernel(
             w4_words.bitcast(I32).rearrange("a p c -> p a c"),
         )
         nc.sync.dma_start(d_sb[:], d.rearrange("(p t) -> p t", t=PACK))
+        nc.sync.dma_start(idx2[:], offs2)
+        nc.sync.dma_start(idx3[:], offs3)
+        load_tab(0)
         for q in range(4):
-            nc.scalar.dma_start(
+            nc.sync.dma_start(
                 w4_sc_raw[32 * q : 32 * q + 4, :].bitcast(I32).rearrange("r (a c) -> r a c", a=PASSES),
                 w4_scales.bitcast(I32)[:, 4 * q : 4 * q + 4, :].rearrange("a r c -> r a c"),
             )
-        load_tab(0)
-        load_tab(1)
-        for a in range(PASSES):
-            nc.sync.dma_start(
-                w1_raw[a][:], w1[512 * a : 512 * (a + 1), :].rearrange("(p j) c -> p j c", j=PACK)
-            )
-        wgs_rows = wgs.rearrange("(q t) j -> q (t j)", t=PACK)
-        for q in (0, 2, 1, 3):
-            nc.sync.dma_start(wgs_first[32 * q : 32 * q + 32, :], wgs_rows[:, 0:S])
-        nc.sync.dma_start(idx2[:], offs2)
-        page_rows = page0.rearrange("(p t) c -> t p c", t=PACK)
-        nc.sync.dma_start(page[0][:], page_rows[0])
-        for q in (0, 2, 1, 3):
-            nc.sync.dma_start(wgs_rest[32 * q : 32 * q + 32, :], wgs_rows[:, S : PACK * S])
-        for t in range(1, PACK):
-            nc.sync.dma_start(page[t][:], page_rows[t])
-        nc.sync.dma_start(idx3[:], offs3)
-        nc.sync.dma_start(wgt_sb[:], wgt)
-        nc.sync.dma_start(w2_raw[:], w2.rearrange("(p j) n -> p j n", j=PACK))
-        nc.sync.dma_start(w5_codes[:].bitcast(I32), w5_words[0].rearrange("p c i -> p (c i)").bitcast(I32))
-        for q in range(4):
-            nc.sync.dma_start(
-                w5_sc[32 * q : 32 * q + 4, :].bitcast(I32), w5_scales[0].bitcast(I32)[4 * q : 4 * q + 4, :]
-            )
-
-        nc.vector.tensor_copy(v_sc_rows[:], tab_sc[:].indirect(idx[:]))
-        for q in range(4):
-            nc.gpsimd.dma_start(
-                v_sc[32 * q : 32 * q + 4, :].bitcast(I32).rearrange("r (a j) -> r a j", a=PASSES),
-                v_sc_rows[8 * q : 8 * q + 8, :].bitcast(I32),
-            )
-        nc.vector.tensor_copy(v_words[0][:], tab[0][:].indirect(idx[:]))
         nc.vector.tensor_copy(
             w4_codes[:].rearrange("p (a t m) -> p a m t", a=PASSES, t=PACK),
             w4_raw[:].rearrange("p (a m t) -> p a m t", a=PASSES, t=PACK),
         )
+        load_tab(1)
+        nc.vector.tensor_copy(v_sc_rows[:], tab_sc[:].indirect(idx[:]))
+        for q in range(4):
+            nc.sync.dma_start(
+                v_sc[32 * q : 32 * q + 4, :].bitcast(I32).rearrange("r (a j) -> r a j", a=PASSES),
+                v_sc_rows[8 * q : 8 * q + 8, :].bitcast(I32),
+            )
+        w1_raw = [placed("w1_raw%d" % a, [P, PACK * H], F32, (32 + 8 * a) * KB) for a in range(PASSES)]
+        for a in range(PASSES):
+            nc.sync.dma_start(
+                w1_raw[a][:], w1[512 * a : 512 * (a + 1), :].rearrange("(p j) c -> p (j c)", j=PACK)
+            )
+        nc.vector.tensor_copy(v_words[0][:], tab[0][:].indirect(idx[:]))
         nc.vector.tensor_copy(
             w4_sc[:].rearrange("p (a t m) -> p a m t", a=PASSES, t=PACK),
             w4_sc_raw[:].rearrange("p (a m t) -> p a m t", a=PASSES, t=PACK),
         )
+        wgs_rows = wgs.rearrange("(q t) j -> q (t j)", t=PACK)
+        wgs_first = swap.tile([P, S], F32, name="wgs_first", offset=EARLY_AT, align_bytes=64)
+        for q in (0, 2, 1, 3):
+            nc.sync.dma_start(wgs_first[32 * q : 32 * q + 32, :], wgs_rows[:, 0:S])
+        page_rows = page0.rearrange("(p t) c -> t p c", t=PACK)
+        page = []
+
+        def load_page(t):
+            page.append(placed("page%d" % t, [P, T2], F32, (0, 8, 32, 40)[t] * KB))
+            nc.sync.dma_start(page[t][:], page_rows[t])
+
+        load_page(0)
+        load_page(1)
         nc.vector.tensor_copy(v_words[1][:], tab[1][:].indirect(idx[:]))
+        wgs_rest = placed("wgs_rest", [P, (PACK - 1) * S], F32, 16 * KB)
+        for q in (0, 2, 1, 3):
+            nc.sync.dma_start(wgs_rest[32 * q : 32 * q + 32, :], wgs_rows[:, S : PACK * S])
+        wgt_sb = placed("wgt_sb", [P, M], F32, 28 * KB)
+        nc.sync.dma_start(wgt_sb[:], wgt)
 
         for a in range(PASSES):
-            nc.vector.tensor_copy(
-                w1_bf[a][:].rearrange("p (t m j) -> p m j t", t=PACK, j=PACK),
-                w1_raw[a][:].rearrange("p j (m t) -> p m j t", t=PACK),
-            )
-            nc.vector.quantize_mx(out=w1_codes[a][:].bitcast(FP8X4), scales=w1_sc[a][:], in_=w1_bf[a][:])
+            dealt = w1_bf[a][:].rearrange("p (t m j) -> p m j t", t=PACK, j=PACK)
+            rows = w1_raw[a][:].rearrange("p (j m t) -> p m j t", j=PACK, t=PACK)
+            if a < PASSES - 1:
+                nc.vector.tensor_copy(dealt, rows)
+            else:
+                nc.vector.tensor_copy(dealt[:, 0:SPLIT], rows[:, 0:SPLIT])
+                nc.scalar.copy(dealt[:, SPLIT:P], rows[:, SPLIT:P])
+            for c0 in range(0, H, H // 2):
+                nc.vector.quantize_mx(
+                    out=w1_codes[a][:, c0 : c0 + H // 2].bitcast(FP8X4),
+                    scales=w1_sc[a][:, c0 : c0 + H // 2],
+                    in_=w1_bf[a][:, PACK * c0 : PACK * (c0 + H // 2)],
+                )
+
+        load_page(2)
+        load_page(3)
+        w2_raw = placed("w2_raw", [P, PACK * N], F32, 48 * KB)
+        nc.sync.dma_start(w2_raw[:], w2.rearrange("(p j) n -> p (j n)", j=PACK))
 
         halves = S // BANK
-        for t in range(PACK):
-            for half in range(halves):
-                acc_b = psum.tile([P, BANK], F32, name="acc_b", tag="second")
-                for a in range(PASSES):
-                    c0 = a * H + t * P
-                    nc.tensor.matmul_mx(
-                        out=acc_b[:],
-                        lhsT=w4_codes[:, c0 : c0 + P].bitcast(FP4X4),
-                        lhsT_scale=w4_sc[:, c0 : c0 + P],
-                        rhs=v_words[a][:, half * BANK : (half + 1) * BANK].bitcast(FP8X4),
-                        rhs_scale=v_sc[:, a * S + half * BANK : a * S + (half + 1) * BANK],
-                        start=(a == 0),
-                        stop=(a == PASSES - 1),
-                    )
-                nc.scalar.copy(b_sb[t * halves + half][:], acc_b[:])
+        units = PACK * halves
 
-        for t in range(PACK):
-            for half in range(halves):
-                acc_a = psum.tile([P, BANK], F32, name="acc_a", tag="first")
-                for a in range(PASSES):
-                    nc.tensor.matmul_mx(
-                        out=acc_a[:],
-                        lhsT=w1_codes[a][:, t * P : (t + 1) * P].bitcast(FP8X4),
-                        lhsT_scale=w1_sc[a][:, t * P : (t + 1) * P],
-                        rhs=v_words[a][:, half * BANK : (half + 1) * BANK].bitcast(FP8X4),
-                        rhs_scale=v_sc[:, a * S + half * BANK : a * S + (half + 1) * BANK],
-                        start=(a == 0),
-                        stop=(a == PASSES - 1),
-                    )
+        def bank(b):
+            return psum.tile([P, BANK], F32, name="bank%d" % b)
+
+        def product_w4(u, acc):
+            t, half = divmod(u, halves)
+            for a in range(PASSES):
+                c0 = a * H + t * P
+                nc.tensor.matmul_mx(
+                    out=acc[:],
+                    lhsT=w4_codes[:, c0 : c0 + P].bitcast(FP4X4),
+                    lhsT_scale=w4_sc[:, c0 : c0 + P],
+                    rhs=v_words[a][:, half * BANK : (half + 1) * BANK].bitcast(FP8X4),
+                    rhs_scale=v_sc[:, a * S + half * BANK : a * S + (half + 1) * BANK],
+                    start=(a == 0),
+                    stop=(a == PASSES - 1),
+                )
+            nc.scalar.copy(b_sb[u][:], acc[:])
+
+        def product_w1(u, acc):
+            t, half = divmod(u, halves)
+            for a in range(PASSES):
+                nc.tensor.matmul_mx(
+                    out=acc[:],
+                    lhsT=w1_codes[a][:, t * P : (t + 1) * P].bitcast(FP8X4),
+                    lhsT_scale=w1_sc[a][:, t * P : (t + 1) * P],
+                    rhs=v_words[a][:, half * BANK : (half + 1) * BANK].bitcast(FP8X4),
+                    rhs_scale=v_sc[:, a * S + half * BANK : a * S + (half + 1) * BANK],
+                    start=(a == 0),
+                    stop=(a == PASSES - 1),
+                )
+            if u < units // 2:
                 larger = ring.tile([P, BANK], F32, name="larger", tag="stage")
-                nc.vector.tensor_tensor(larger[:], acc_a[:], b_sb[t * halves + half][:], MAX)
-                c0 = t * S + half * BANK
-                nc.scalar.activation(h_sb[:, c0 : c0 + BANK], larger[:], IDENTITY, bias=d_sb[:, t : t + 1])
+            else:
+                larger = swap.tile(
+                    [P, BANK], F32, name="larger%d" % half, offset=EARLY_AT + 4 * BANK * half, align_bytes=64
+                )
+            nc.vector.tensor_tensor(larger[:], acc[:], b_sb[u][:], MAX)
+            c0 = t * S + half * BANK
+            nc.scalar.activation(h_sb[:, c0 : c0 + BANK], larger[:], IDENTITY, bias=d_sb[:, t : t + 1])
 
-        for t in range(PACK):
+        for u in range(units // 2):
+            product_w4(u, bank(u))
+        for u in range(units // 2):
+            product_w1(u, bank(units // 2 + u))
+
+        def put(t):
             weight = wgs_first[:] if t == 0 else wgs_rest[:, (t - 1) * S : t * S]
             nc.vector.tensor_tensor(page[t][:].indirect(idx2[:]), h_sb[:, t * S : (t + 1) * S], weight, MULT)
 
+        put(0)
+        for u in range(units // 2, units):
+            product_w4(u, bank(u))
+            product_w1(u, bank(u))
+        for t in range(1, PACK):
+            put(t)
+
+        w5_codes = placed("w5_codes", [P, N], U32, 56 * KB)
+        w5_sc = placed("w5_sc", [P, N], U8, 58 * KB)
+        nc.sync.dma_start(w5_codes[:].bitcast(I32), w5_words[0].rearrange("p c i -> p (c i)").bitcast(I32))
+        nc.vector.memset(w5_sc[:].bitcast(I32), 0)
+        for q in range(4):
+            nc.sync.dma_start(
+                w5_sc[32 * q : 32 * q + 4, :].bitcast(I32), w5_scales[0].bitcast(I32)[4 * q : 4 * q + 4, :]
+            )
         nc.scalar.copy(
             w2_bf[:].rearrange("p (c i j) -> p c j i", i=4, j=PACK),
-            w2_raw[:].rearrange("p j (c i) -> p c j i", i=4),
+            w2_raw[:].rearrange("p (j c i) -> p c j i", i=4, j=PACK),
         )
         nc.vector.quantize_mx(out=w2_codes[:].bitcast(FP8X4), scales=w2_sc[:], in_=w2_bf[:])
 
         out_rows = out.rearrange("(g p) m -> p g m", p=P)
         m0 = 0
         for c, width in enumerate(CHUNKS):
-            picked = swap.tile([P, PACK, width], F32, name="picked%d" % c, offset=4 * PACK * m0)
+            picked = swap.tile([P, PACK, width], F32, name="picked%d" % c, offset=PICKED_AT[c], align_bytes=64)
             for t in range(PACK):
                 nc.vector.tensor_tensor(
                     picked[:, t, :],
@@ -198,7 +240,7 @@ def tile_list_corridor_cell_limits_kernel(
                     wgt_sb[:, m0 : m0 + width],
                     MULT,
                 )
-            x_bf = held("x_bf%d" % c, [P, PACK * width], BF16)
+            x_bf = swap.tile([P, PACK * width], BF16, name="x_bf%d" % c, offset=XBF_AT[c], align_bytes=64)
             nc.scalar.copy(
                 x_bf[:].rearrange("p (c i t) -> p c t i", i=4, t=PACK),
                 picked[:].rearrange("p t (c i) -> p c t i", i=4),
@@ -208,8 +250,8 @@ def tile_list_corridor_cell_limits_kernel(
             nc.vector.quantize_mx(out=x_codes[:].bitcast(FP8X4), scales=x_sc[:], in_=x_bf[:])
             per_bank = BANK // width
             for g0 in range(0, N // P, per_bank):
-                acc_c = psum.tile([P, BANK], F32, name="acc_c", tag="first")
-                acc_e = psum.tile([P, BANK], F32, name="acc_e", tag="second")
+                acc_c = bank((4 * c + g0) % 8)
+                acc_e = bank((4 * c + g0 + 1) % 8)
                 for acc, codes, scales in ((acc_e, w5_codes, w5_sc), (acc_c, w2_codes, w2_sc)):
                     for g in range(per_bank):
                         n0 = (g0 + g) * P

from contextlib import ExitStack

import concourse.mybir as mybir

K, T, S, H, T2, M, N = 1024, 4096, 1024, 512, 2048, 1024, 512
FLOPS = 2 * (2 * K * H * S + 2 * H * N * M)

F32 = mybir.dt.float32
BF16 = mybir.dt.bfloat16
I32 = mybir.dt.int32
U32 = mybir.dt.uint32
U16 = mybir.dt.uint16
U8 = mybir.dt.uint8
FP8X4 = mybir.dt.float8_e4m3fn_x4
FP4X4 = mybir.dt.float4_e2m1fn_x4
MULT = mybir.AluOpType.mult
MAX = mybir.AluOpType.max
IDENTITY = mybir.ActivationFunctionType.Identity

P = 128
PACK = 4
PASSES = K // (P * PACK)
BANK = 512
CHUNKS = (256, 256, 256, 256)
PICKED_AT = (0, 4096, 8192, 12288)
XBF_AT = (16384, 12288, 18432, 20480)
EARLY_AT = 22528
SPLIT = 88
KB = 1024


def tile_list_corridor_cell_limits_kernel(
    tc, tab_words, tab_scales, offs, w1, w4_words, w4_scales, d, page0, wgs, offs2, wgt, offs3,
    w2, w5_words, w5_scales, out,
):
    nc = tc.nc
    with ExitStack() as ctx:
        keep = ctx.enter_context(tc.tile_pool(name="keep", bufs=1))
        swap = ctx.enter_context(tc.tile_pool(name="swap", bufs=1))
        reuse = ctx.enter_context(tc.tile_pool(name="reuse", bufs=1))
        ring = ctx.enter_context(tc.tile_pool(name="ring", bufs=3))
        outs = ctx.enter_context(tc.tile_pool(name="outs", bufs=8))
        psum = ctx.enter_context(tc.psum_pool(name="psum", bufs=1))

        def held(name, shape, dtype):
            return keep.tile(shape, dtype, name=name, align_bytes=64)

        idx = held("idx", [P, S // 16], U16)
        idx2 = held("idx2", [P, S // 16], U16)
        idx3 = held("idx3", [P, M // 16], U16)
        def placed(name, shape, dtype, offset):
            return reuse.tile(shape, dtype, name=name, align_bytes=64, offset=offset)

        tab = [placed("tab%d" % a, [P, T], U32, 4 * T * a) for a in range(PASSES)]
        tab_sc = placed("tab_sc", [P, T], U8, 38 * KB)
        v_words = [held("v_words%d" % a, [P, S], U32) for a in range(PASSES)]
        v_sc_rows = held("v_sc_rows", [P, S], U8)
        v_sc = held("v_sc", [P, PASSES * S], U8)
        w4_raw = placed("w4_raw", [P, PASSES * H], U16, 4 * T)
        w4_sc_raw = swap.tile([P, PASSES * H], U8, name="w4_sc_raw", offset=EARLY_AT, align_bytes=64)
        w4_codes = placed("w4_codes", [P, PASSES * H], U16, 56 * KB)
        w4_sc = placed("w4_sc", [P, PASSES * H], U8, 58 * KB)
        w1_bf = [placed("w1_bf%d" % a, [P, PACK * H], BF16, (48 + 4 * a) * KB) for a in range(PASSES)]
        w1_codes = [held("w1_codes%d" % a, [P, H], U32) for a in range(PASSES)]
        w1_sc = [held("w1_sc%d" % a, [P, H], U8) for a in range(PASSES)]
        d_sb = held("d_sb", [P, PACK], F32)
        w2_bf = held("w2_bf", [P, PACK * N], BF16)
        w2_codes = held("w2_codes", [P, N], U32)
        w2_sc = held("w2_sc", [P, N], U8)
        b_sb = [held("b_sb%d" % u, [P, BANK], F32) for u in range(PACK * S // BANK)]
        h_sb = swap.tile([P, PACK * S], F32, name="h_sb", offset=0, align_bytes=64)

        nc.vector.memset(w4_sc_raw[:].bitcast(I32), 0)
        nc.vector.memset(tab_sc[32:64, :].bitcast(I32), 0)
        nc.vector.memset(tab_sc[64:128, :].bitcast(I32), 0)
        nc.vector.memset(v_sc[:].bitcast(I32), 0)

        def load_tab(a):
            nc.sync.dma_start(tab[a][:].bitcast(I32), tab_words[a].rearrange("p t i -> p (t i)").bitcast(I32))

        nc.sync.dma_start(idx[:], offs)
        nc.sync.dma_start(
            tab_sc[0:32, :].bitcast(I32), tab_scales.bitcast(I32).rearrange("a q t -> q a t")
        )
        nc.sync.dma_start(
            w4_raw[:].bitcast(I32).rearrange("p (a c) -> p a c", a=PASSES),
            w4_words.bitcast(I32).rearrange("a p c -> p a c"),
        )
        nc.sync.dma_start(d_sb[:], d.rearrange("(p t) -> p t", t=PACK))
        nc.sync.dma_start(idx2[:], offs2)
        nc.sync.dma_start(idx3[:], offs3)
        load_tab(0)
        for q in range(4):
            nc.sync.dma_start(
                w4_sc_raw[32 * q : 32 * q + 4, :].bitcast(I32).rearrange("r (a c) -> r a c", a=PASSES),
                w4_scales.bitcast(I32)[:, 4 * q : 4 * q + 4, :].rearrange("a r c -> r a c"),
            )
        nc.vector.tensor_copy(
            w4_codes[:].rearrange("p (a t m) -> p a m t", a=PASSES, t=PACK),
            w4_raw[:].rearrange("p (a m t) -> p a m t", a=PASSES, t=PACK),
        )
        load_tab(1)
        nc.vector.tensor_copy(v_sc_rows[:], tab_sc[:].indirect(idx[:]))
        for q in range(4):
            nc.sync.dma_start(
                v_sc[32 * q : 32 * q + 4, :].bitcast(I32).rearrange("r (a j) -> r a j", a=PASSES),
                v_sc_rows[8 * q : 8 * q + 8, :].bitcast(I32),
            )
        w1_raw = [placed("w1_raw%d" % a, [P, PACK * H], F32, (32 + 8 * a) * KB) for a in range(PASSES)]
        for a in range(PASSES):
            nc.sync.dma_start(
                w1_raw[a][:], w1[512 * a : 512 * (a + 1), :].rearrange("(p j) c -> p (j c)", j=PACK)
            )
        nc.vector.tensor_copy(v_words[0][:], tab[0][:].indirect(idx[:]))
        nc.vector.tensor_copy(
            w4_sc[:].rearrange("p (a t m) -> p a m t", a=PASSES, t=PACK),
            w4_sc_raw[:].rearrange("p (a m t) -> p a m t", a=PASSES, t=PACK),
        )
        wgs_rows = wgs.rearrange("(q t) j -> q (t j)", t=PACK)
        wgs_first = swap.tile([P, S], F32, name="wgs_first", offset=EARLY_AT, align_bytes=64)
        for q in (0, 2, 1, 3):
            nc.sync.dma_start(wgs_first[32 * q : 32 * q + 32, :], wgs_rows[:, 0:S])
        page_rows = page0.rearrange("(p t) c -> t p c", t=PACK)
        page = []

        def load_page(t):
            page.append(placed("page%d" % t, [P, T2], F32, (0, 8, 32, 40)[t] * KB))
            nc.sync.dma_start(page[t][:], page_rows[t])

        load_page(0)
        load_page(1)
        nc.vector.tensor_copy(v_words[1][:], tab[1][:].indirect(idx[:]))
        wgs_rest = placed("wgs_rest", [P, (PACK - 1) * S], F32, 16 * KB)
        for q in (0, 2, 1, 3):
            nc.sync.dma_start(wgs_rest[32 * q : 32 * q + 32, :], wgs_rows[:, S : PACK * S])
        wgt_sb = placed("wgt_sb", [P, M], F32, 28 * KB)
        nc.sync.dma_start(wgt_sb[:], wgt)

        for a in range(PASSES):
            dealt = w1_bf[a][:].rearrange("p (t m j) -> p m j t", t=PACK, j=PACK)
            rows = w1_raw[a][:].rearrange("p (j m t) -> p m j t", j=PACK, t=PACK)
            if a < PASSES - 1:
                nc.vector.tensor_copy(dealt, rows)
            else:
                nc.vector.tensor_copy(dealt[:, 0:SPLIT], rows[:, 0:SPLIT])
                nc.scalar.copy(dealt[:, SPLIT:P], rows[:, SPLIT:P])
            for c0 in range(0, H, H // 2):
                nc.vector.quantize_mx(
                    out=w1_codes[a][:, c0 : c0 + H // 2].bitcast(FP8X4),
                    scales=w1_sc[a][:, c0 : c0 + H // 2],
                    in_=w1_bf[a][:, PACK * c0 : PACK * (c0 + H // 2)],
                )

        load_page(2)
        load_page(3)
        w2_raw = placed("w2_raw", [P, PACK * N], F32, 48 * KB)
        nc.sync.dma_start(w2_raw[:], w2.rearrange("(p j) n -> p (j n)", j=PACK))

        halves = S // BANK
        units = PACK * halves

        def bank(b):
            return psum.tile([P, BANK], F32, name="bank%d" % b)

        def product_w4(u, acc):
            t, half = divmod(u, halves)
            for a in range(PASSES):
                c0 = a * H + t * P
                nc.tensor.matmul_mx(
                    out=acc[:],
                    lhsT=w4_codes[:, c0 : c0 + P].bitcast(FP4X4),
                    lhsT_scale=w4_sc[:, c0 : c0 + P],
                    rhs=v_words[a][:, half * BANK : (half + 1) * BANK].bitcast(FP8X4),
                    rhs_scale=v_sc[:, a * S + half * BANK : a * S + (half + 1) * BANK],
                    start=(a == 0),
                    stop=(a == PASSES - 1),
                )
            nc.scalar.copy(b_sb[u][:], acc[:])

        def product_w1(u, acc):
            t, half = divmod(u, halves)
            for a in range(PASSES):
                nc.tensor.matmul_mx(
                    out=acc[:],
                    lhsT=w1_codes[a][:, t * P : (t + 1) * P].bitcast(FP8X4),
                    lhsT_scale=w1_sc[a][:, t * P : (t + 1) * P],
                    rhs=v_words[a][:, half * BANK : (half + 1) * BANK].bitcast(FP8X4),
                    rhs_scale=v_sc[:, a * S + half * BANK : a * S + (half + 1) * BANK],
                    start=(a == 0),
                    stop=(a == PASSES - 1),
                )
            if u < units // 2:
                larger = ring.tile([P, BANK], F32, name="larger", tag="stage")
            else:
                larger = swap.tile(
                    [P, BANK], F32, name="larger%d" % half, offset=EARLY_AT + 4 * BANK * half, align_bytes=64
                )
            nc.vector.tensor_tensor(larger[:], acc[:], b_sb[u][:], MAX)
            c0 = t * S + half * BANK
            nc.scalar.activation(h_sb[:, c0 : c0 + BANK], larger[:], IDENTITY, bias=d_sb[:, t : t + 1])

        for u in range(units // 2):
            product_w4(u, bank(u))
        for u in range(units // 2):
            product_w1(u, bank(units // 2 + u))

        def put(t):
            weight = wgs_first[:] if t == 0 else wgs_rest[:, (t - 1) * S : t * S]
            nc.vector.tensor_tensor(page[t][:].indirect(idx2[:]), h_sb[:, t * S : (t + 1) * S], weight, MULT)

        put(0)
        for u in range(units // 2, units):
            product_w4(u, bank(u))
            product_w1(u, bank(u))
        for t in range(1, PACK):
            put(t)

        w5_codes = placed("w5_codes", [P, N], U32, 56 * KB)
        w5_sc = placed("w5_sc", [P, N], U8, 58 * KB)
        nc.sync.dma_start(w5_codes[:].bitcast(I32), w5_words[0].rearrange("p c i -> p (c i)").bitcast(I32))
        nc.vector.memset(w5_sc[:].bitcast(I32), 0)
        for q in range(4):
            nc.sync.dma_start(
                w5_sc[32 * q : 32 * q + 4, :].bitcast(I32), w5_scales[0].bitcast(I32)[4 * q : 4 * q + 4, :]
            )
        nc.scalar.copy(
            w2_bf[:].rearrange("p (c i j) -> p c j i", i=4, j=PACK),
            w2_raw[:].rearrange("p (j c i) -> p c j i", i=4, j=PACK),
        )
        nc.vector.quantize_mx(out=w2_codes[:].bitcast(FP8X4), scales=w2_sc[:], in_=w2_bf[:])

        out_rows = out.rearrange("(g p) m -> p g m", p=P)
        m0 = 0
        for c, width in enumerate(CHUNKS):
            picked = swap.tile([P, PACK, width], F32, name="picked%d" % c, offset=PICKED_AT[c], align_bytes=64)
            for t in range(PACK):
                nc.vector.tensor_tensor(
                    picked[:, t, :],
                    page[t][:].indirect(idx3[:, m0 // 16 : (m0 + width) // 16]),
                    wgt_sb[:, m0 : m0 + width],
                    MULT,
                )
            x_bf = swap.tile([P, PACK * width], BF16, name="x_bf%d" % c, offset=XBF_AT[c], align_bytes=64)
            nc.scalar.copy(
                x_bf[:].rearrange("p (c i t) -> p c t i", i=4, t=PACK),
                picked[:].rearrange("p t (c i) -> p c t i", i=4),
            )
            x_codes = held("x_codes%d" % c, [P, width], U32)
            x_sc = held("x_sc%d" % c, [P, width], U8)
            nc.vector.quantize_mx(out=x_codes[:].bitcast(FP8X4), scales=x_sc[:], in_=x_bf[:])
            per_bank = BANK // width
            for g0 in range(0, N // P, per_bank):
                acc_c = bank((4 * c + g0) % 8)
                acc_e = bank((4 * c + g0 + 1) % 8)
                for acc, codes, scales in ((acc_e, w5_codes, w5_sc), (acc_c, w2_codes, w2_sc)):
                    for g in range(per_bank):
                        n0 = (g0 + g) * P
                        nc.tensor.matmul_mx(
                            out=acc[:, g * width : (g + 1) * width],
                            lhsT=codes[:, n0 : n0 + P].bitcast(FP8X4),
                            lhsT_scale=scales[:, n0 : n0 + P],
                            rhs=x_codes[:].bitcast(FP8X4),
                            rhs_scale=x_sc[:],
                            start=True,
                            stop=True,
                        )
                e_sb = ring.tile([P, BANK], F32, name="e_sb", tag="stage")
                nc.scalar.copy(e_sb[:], acc_e[:])
                result = outs.tile([P, BANK], F32, name="result")
                nc.vector.tensor_tensor(result[:], acc_c[:], e_sb[:], MAX)
                nc.sync.dma_start(
                    out_rows[:, g0 : g0 + per_bank, m0 : m0 + width],
                    result[:].rearrange("p (g m) -> p g m", g=per_bank),
                )
            m0 += width
